import numpy as np
import ml_dtypes


def mxq(x, axis, fmt="e4m3"):
    dtype, down = {"e4m3": (ml_dtypes.float8_e4m3fn, 7), "e5m2": (ml_dtypes.float8_e5m2, 14)}[fmt]
    v = np.moveaxis(np.asarray(x, np.float32).astype(ml_dtypes.bfloat16).astype(np.float64), axis, -1)
    blocks = v.reshape(v.shape[:-1] + (-1, 32))
    amax = np.abs(blocks).max(-1, keepdims=True)
    byte = np.maximum(np.where(amax > 0, np.frexp(amax)[1] - 1 + 127, 0) - down, 1)
    scale = np.exp2(byte - 127.0)
    codes = (blocks / scale).astype(np.float32).astype(dtype).astype(np.float64)
    return np.moveaxis((codes * scale).reshape(v.shape), -1, axis)


WIDE = False


def mx_kscale(k):
    if not WIDE:
        return np.ones(k)
    levels = np.array([10, -10, 5, -5, 0])
    if k % 512:
        return np.exp2(np.random.permutation(np.resize(levels, k // 32))).repeat(32)
    a = np.empty((k // 512, 16))
    for p in range(k // 512):
        a[p, :8] = np.random.permutation(np.resize(levels, 8))
        for g in range(8):
            far = levels[np.abs(levels - a[p, g]) >= 10]
            a[p, g + 8] = far[np.random.randint(len(far))]
    return np.exp2(a.ravel()).repeat(32)


BF16 = ml_dtypes.bfloat16


def bf(x):
    return np.asarray(x, np.float32).astype(BF16)


def f64(x):
    return np.asarray(x).astype(np.float64)


E2M1 = np.array([0.0, 0.5, 1.0, 1.5, 2.0, 3.0, 4.0, 6.0, -0.0, -0.5, -1.0, -1.5, -2.0, -3.0, -4.0, -6.0])


def pack_weight(w, fmt):
    k, n = w.shape
    w = f64(bf(w)).reshape(k // 32, 32, n)
    amax = np.abs(w).max(1)
    if fmt == "e4m3":
        byte = np.frexp(amax)[1] - 1 + 127 - 7
    else:
        mant, ex = np.frexp(amax / 6.0)
        byte = np.where(mant > 0.5, ex, ex - 1) + 127
    byte = np.clip(np.where(amax > 0, byte, 1), 1, 254)
    scaled = (w * np.exp2(127.0 - byte)[:, None, :]).reshape(k, n).astype(np.float32)
    by_word = np.ascontiguousarray(scaled.reshape(k // 512, 128, 4, n).transpose(0, 1, 3, 2))
    if fmt == "e4m3":
        words = by_word.astype(ml_dtypes.float8_e4m3fn).view(np.uint8)
    else:
        c = by_word.astype(ml_dtypes.float4_e2m1fn).view(np.uint8) & 0xF
        words = c[..., 0::2] | (c[..., 1::2] << 4)
    return np.ascontiguousarray(words), np.ascontiguousarray(byte.astype(np.uint8).reshape(k // 512, 16, n))


def unpack_weight(words, scales, fmt):
    g, p, n, _ = words.shape
    if fmt == "e4m3":
        vals = np.ascontiguousarray(words).view(ml_dtypes.float8_e4m3fn).astype(np.float64)
    else:
        nib = np.empty((g, p, n, 4), np.uint8)
        nib[..., 0::2] = words & 0xF
        nib[..., 1::2] = words >> 4
        vals = E2M1[nib]
    vals = vals * np.repeat(np.exp2(scales.astype(np.float64) - 127.0), 8, axis=1)[..., None]
    return vals.transpose(0, 1, 3, 2).reshape(g * 512, n)
def pack4(w):
    words, scales = pack_weight(w, "e2m1")
    return words.reshape(words.shape[0], 128, -1), scales


def unpack4(words, scales):
    return unpack_weight(words.reshape(words.shape[0], 128, -1, 2), scales, "e2m1")


def planes(Y):
    n, m = Y.shape
    b = f64(bf(Y)).reshape(n // 32, 32, m)
    amax = np.abs(b).max(1)
    byte = np.clip(np.where(amax > 0, np.frexp(amax)[1] - 1 + 127 - 7, 1), 1, 254)
    codes = (b * np.exp2(127.0 - byte)[:, None, :]).reshape(n, m).astype(np.float32).astype(ml_dtypes.float8_e4m3fn).view(np.uint8)
    words = codes.reshape(n // 512, 128, 4, m).transpose(0, 1, 3, 2)
    return np.ascontiguousarray(words), np.ascontiguousarray(byte.astype(np.uint8).reshape(n // 512, 16, m))


M, N = 1024, 1536


def setup_inputs():
    s = mx_kscale(M)
    t = mx_kscale(N)
    right = np.random.randn(N, N) / np.sqrt(N) / t[:, None]
    right_words, right_scales = pack4(right)
    return {
        "grad": bf(np.random.randn(M, N)),
        "row_scale": bf(np.exp(0.3 * np.random.randn(M)) * s),
        "left_t": bf(np.random.randn(M, M) / np.sqrt(M) / s[:, None]),
        "col_scale": bf(np.exp(0.3 * np.random.randn(N)) * t),
        "right_words": right_words,
        "right_scales": right_scales,
        "diag_gain": bf(1.0 + 0.1 * np.random.randn(N)),
        "trust": bf(0.5 * np.exp(0.8 * np.random.randn(M))),
    }


def reference(grad, row_scale, left_t, col_scale, right_words, right_scales, diag_gain, trust):
    G = f64(grad)
    X = f64(row_scale)[:, None] * G
    Z = G * f64(col_scale)[None, :]
    left = mxq(f64(left_t), 0, "e4m3").T @ mxq(X, 0, "e4m3")
    right = mxq(Z, 1, "e4m3") @ unpack4(right_words, right_scales)
    y = f64(trust)[:, None] * (left + right + G * f64(diag_gain)[None, :])
    Y = y.reshape(M, N)
    words, scales = planes(Y)
    return y, words, scales

@@ -1,0 +1,558 @@
+from contextlib import ExitStack
+
+import concourse.mybir as mybir
+from concourse.masks import make_identity
+
+M, N = 1024, 1536
+FLOPS = 2 * M * M * N + 2 * M * N * N
+
+F32 = mybir.dt.float32
+BF16 = mybir.dt.bfloat16
+I32 = mybir.dt.int32
+U32 = mybir.dt.uint32
+U8 = mybir.dt.uint8
+FP8X4 = mybir.dt.float8_e4m3fn_x4
+FP4X4 = mybir.dt.float4_e2m1fn_x4
+ALU = mybir.AluOpType
+ACT = mybir.ActivationFunctionType
+
+P = 128
+PACK = 4
+W = 512
+GROUPS = M // W
+CHUNKS = N // W
+ACC_BANKS = 6
+TURN_BANKS = 2
+
+ORDER = [('ident',),
+    ('ld', ('v', 'diag'), 'S'),
+    ('ld', ('v', 'row'), 'S'),
+    ('ld', ('v', 'col'), 'S'),
+    ('ld', ('v', 'trust'), 'S'),
+    ('ld', ('G', 0, 0)),
+    ('ld', ('G', 0, 1)),
+    ('ld', ('L', 0, 0)),
+    ('ld', ('G', 1, 0)),
+    ('memset',),
+    ('ld', ('G', 0, 2)),
+    ('ld', ('R', 0)),
+    ('ld', ('rs',)),
+    ('ld', ('L', 1, 0)),
+    ('ld', ('G', 1, 1)),
+    ('ld', ('R', 1)),
+    ('ld', ('G', 1, 2)),
+    ('ld', ('L', 0, 1)),
+    ('ld', ('L', 1, 1)),
+    ('ld', ('R', 2)),
+    ('TD', 0),
+    ('ED', 0),
+    ('TD', 1),
+    ('ED', 1),
+    ('rowf',),
+    ('Xs', 0, 0),
+    ('T', 0, 0, 0),
+    ('T', 0, 0, 1),
+    ('Xi', 0, 0),
+    ('A', 0, 0, 0),
+    ('Zm', 0, 0, 0),
+    ('Zm', 0, 0, 1),
+    ('T', 0, 1, 0),
+    ('T', 0, 1, 1),
+    ('Li', 0, 0),
+    ('Xs', 1, 0),
+    ('Zq', 0, 0),
+    ('Zm', 0, 1, 0),
+    ('Zm', 0, 1, 1),
+    ('Xq', 0, 0),
+    ('Xi', 1, 0),
+    ('T', 0, 2, 0),
+    ('T', 0, 2, 1),
+    ('Zq', 0, 1),
+    ('Zm', 0, 2, 0),
+    ('Zm', 0, 2, 1),
+    ('Lq', 0, 0),
+    ('M', 0, 0, 0, 0),
+    ('M', 0, 0, 1, 0),
+    ('M', 0, 0, 2, 0),
+    ('M', 0, 0, 3, 0),
+    ('M', 0, 0, 0, 1),
+    ('M', 0, 0, 1, 1),
+    ('M', 0, 0, 2, 1),
+    ('M', 0, 0, 3, 1),
+    ('Li', 1, 0),
+    ('Zq', 0, 2),
+    ('Xs', 0, 1),
+    ('Xi', 0, 1),
+    ('A', 0, 0, 1),
+    ('M', 0, 0, 0, 3),
+    ('M', 0, 0, 1, 3),
+    ('M', 0, 0, 2, 3),
+    ('M', 0, 0, 3, 3),
+    ('M', 0, 0, 0, 2),
+    ('M', 0, 0, 1, 2),
+    ('M', 0, 0, 2, 2),
+    ('M', 0, 0, 3, 2),
+    ('T', 1, 0, 0),
+    ('T', 1, 0, 1),
+    ('Xq', 1, 0),
+    ('A', 0, 0, 2),
+    ('Xs', 1, 1),
+    ('Xi', 1, 1),
+    ('Lq', 1, 0),
+    ('A', 0, 0, 3),
+    ('M', 0, 1, 0, 0),
+    ('M', 0, 1, 0, 1),
+    ('M', 0, 1, 0, 2),
+    ('M', 0, 1, 1, 0),
+    ('M', 0, 1, 1, 1),
+    ('M', 0, 1, 1, 2),
+    ('M', 0, 0, 0, 4),
+    ('M', 0, 0, 1, 4),
+    ('M', 0, 0, 2, 4),
+    ('M', 0, 0, 3, 4),
+    ('Zm', 1, 0, 0),
+    ('Zm', 1, 0, 1),
+    ('Xq', 0, 1),
+    ('T', 1, 1, 0),
+    ('T', 1, 1, 1),
+    ('Xs', 0, 2, 'S'),
+    ('Xi', 0, 2),
+    ('B', 0, 0, 0),
+    ('sy', 0, 0, 0),
+    ('A', 0, 1, 0),
+    ('B', 0, 0, 1),
+    ('sy', 0, 0, 1),
+    ('Xq', 1, 1),
+    ('M', 0, 1, 0, 3),
+    ('M', 0, 1, 1, 3),
+    ('M', 0, 1, 0, 4),
+    ('M', 0, 1, 1, 4),
+    ('M', 0, 1, 2, 0),
+    ('M', 0, 1, 2, 1),
+    ('M', 0, 1, 2, 2),
+    ('M', 0, 1, 2, 3),
+    ('M', 0, 1, 2, 4),
+    ('B', 0, 0, 2),
+    ('sy', 0, 0, 2),
+    ('A', 0, 1, 1),
+    ('B', 0, 0, 3),
+    ('sy', 0, 0, 3),
+    ('M', 0, 1, 3, 0),
+    ('M', 0, 1, 3, 1),
+    ('M', 0, 1, 3, 2),
+    ('M', 0, 1, 3, 3),
+    ('M', 0, 1, 3, 4),
+    ('Zq', 1, 0),
+    ('Xs', 1, 2, 'S'),
+    ('Xi', 1, 2),
+    ('Zm', 1, 1, 0),
+    ('Zm', 1, 1, 1),
+    ('T', 1, 2, 0),
+    ('T', 1, 2, 1),
+    ('B', 0, 1, 0),
+    ('sy', 0, 1, 0),
+    ('Xq', 0, 2),
+    ('B', 0, 1, 1),
+    ('sy', 0, 1, 1),
+    ('A', 0, 1, 2),
+    ('M', 0, 2, 0, 0),
+    ('M', 0, 2, 0, 1),
+    ('M', 0, 2, 0, 2),
+    ('M', 0, 2, 0, 3),
+    ('M', 0, 2, 1, 0),
+    ('M', 0, 2, 1, 1),
+    ('M', 0, 2, 1, 2),
+    ('M', 0, 2, 1, 3),
+    ('Zq', 1, 1),
+    ('B', 0, 1, 2),
+    ('sy', 0, 1, 2),
+    ('A', 0, 1, 3),
+    ('M', 0, 2, 2, 0),
+    ('M', 0, 2, 2, 1),
+    ('M', 0, 2, 2, 2),
+    ('M', 0, 2, 2, 3),
+    ('Zm', 1, 2, 0),
+    ('B', 0, 1, 3),
+    ('sy', 0, 1, 3),
+    ('Zm', 1, 2, 1),
+    ('Li', 0, 1),
+    ('Xq', 1, 2),
+    ('M', 0, 2, 3, 0),
+    ('M', 0, 2, 3, 1),
+    ('M', 0, 2, 3, 2),
+    ('M', 0, 2, 3, 3),
+    ('M', 0, 2, 0, 4),
+    ('M', 0, 2, 1, 4),
+    ('M', 0, 2, 2, 4),
+    ('M', 0, 2, 3, 4),
+    ('A', 0, 2, 0),
+    ('Zq', 1, 2),
+    ('A', 0, 2, 1),
+    ('Li', 1, 1),
+    ('Lq', 0, 1),
+    ('M', 1, 0, 0, 0),
+    ('M', 1, 0, 0, 1),
+    ('M', 1, 0, 0, 2),
+    ('M', 1, 0, 0, 3),
+    ('M', 1, 0, 1, 0),
+    ('M', 1, 0, 1, 1),
+    ('M', 1, 0, 1, 2),
+    ('M', 1, 0, 1, 3),
+    ('B', 0, 2, 0),
+    ('sy', 0, 2, 0),
+    ('A', 0, 2, 2),
+    ('B', 0, 2, 1),
+    ('sy', 0, 2, 1),
+    ('Lq', 1, 1),
+    ('Yi', 0, 0, 0, 1),
+    ('M', 1, 0, 0, 4),
+    ('M', 1, 0, 1, 4),
+    ('M', 1, 0, 2, 0),
+    ('M', 1, 0, 2, 1),
+    ('M', 1, 0, 2, 2),
+    ('M', 1, 0, 2, 3),
+    ('M', 1, 0, 2, 4),
+    ('A', 0, 2, 3),
+    ('B', 0, 2, 2),
+    ('sy', 0, 2, 2),
+    ('A', 1, 0, 0),
+    ('B', 0, 2, 3),
+    ('sy', 0, 2, 3),
+    ('M', 1, 0, 3, 0),
+    ('M', 1, 0, 3, 1),
+    ('M', 1, 0, 3, 2),
+    ('M', 1, 0, 3, 3),
+    ('M', 1, 0, 3, 4),
+    ('Yi', 0, 1, 0, 1),
+    ('Yi', 0, 2, 0, 1),
+    ('A', 1, 0, 1),
+    ('B', 1, 0, 0),
+    ('sy', 1, 0, 0),
+    ('M', 1, 1, 0, 0),
+    ('M', 1, 1, 0, 1),
+    ('M', 1, 1, 0, 2),
+    ('M', 1, 1, 0, 3),
+    ('M', 1, 1, 0, 4),
+    ('A', 1, 0, 2),
+    ('Yq', 0, 0, 0, 1),
+    ('sw', 0, 0, 0, 1),
+    ('B', 1, 0, 1),
+    ('sy', 1, 0, 1),
+    ('M', 1, 1, 1, 0),
+    ('M', 1, 1, 1, 1),
+    ('M', 1, 1, 1, 2),
+    ('M', 1, 1, 1, 3),
+    ('M', 1, 1, 1, 4),
+    ('A', 1, 0, 3),
+    ('B', 1, 0, 2),
+    ('sy', 1, 0, 2),
+    ('M', 1, 1, 2, 0),
+    ('M', 1, 1, 2, 1),
+    ('M', 1, 1, 2, 2),
+    ('M', 1, 1, 2, 3),
+    ('M', 1, 1, 2, 4),
+    ('A', 1, 1, 0),
+    ('B', 1, 0, 3),
+    ('sy', 1, 0, 3),
+    ('M', 1, 1, 3, 0),
+    ('M', 1, 1, 3, 1),
+    ('M', 1, 1, 3, 2),
+    ('M', 1, 1, 3, 3),
+    ('M', 1, 1, 3, 4),
+    ('Yi', 1, 0, 0, 1),
+    ('A', 1, 1, 1),
+    ('B', 1, 1, 0),
+    ('sy', 1, 1, 0),
+    ('M', 1, 2, 0, 0),
+    ('M', 1, 2, 0, 1),
+    ('M', 1, 2, 0, 2),
+    ('M', 1, 2, 0, 3),
+    ('M', 1, 2, 0, 4),
+    ('A', 1, 1, 2),
+    ('Yq', 0, 1, 0, 1),
+    ('sw', 0, 1, 0, 1),
+    ('B', 1, 1, 1),
+    ('sy', 1, 1, 1),
+    ('M', 1, 2, 1, 0),
+    ('M', 1, 2, 1, 1),
+    ('M', 1, 2, 1, 2),
+    ('M', 1, 2, 1, 3),
+    ('M', 1, 2, 1, 4),
+    ('A', 1, 1, 3),
+    ('B', 1, 1, 2),
+    ('sy', 1, 1, 2),
+    ('M', 1, 2, 2, 0),
+    ('M', 1, 2, 2, 1),
+    ('M', 1, 2, 2, 2),
+    ('M', 1, 2, 2, 3),
+    ('M', 1, 2, 2, 4),
+    ('A', 1, 2, 0),
+    ('B', 1, 1, 3),
+    ('sy', 1, 1, 3),
+    ('M', 1, 2, 3, 0),
+    ('M', 1, 2, 3, 1),
+    ('M', 1, 2, 3, 2),
+    ('M', 1, 2, 3, 3),
+    ('M', 1, 2, 3, 4),
+    ('Yi', 1, 1, 0, 1),
+    ('A', 1, 2, 1),
+    ('B', 1, 2, 0),
+    ('sy', 1, 2, 0),
+    ('A', 1, 2, 2),
+    ('Yq', 0, 2, 0, 1),
+    ('sw', 0, 2, 0, 1),
+    ('B', 1, 2, 1),
+    ('sy', 1, 2, 1),
+    ('A', 1, 2, 3),
+    ('ss', 0),
+    ('B', 1, 2, 2),
+    ('sy', 1, 2, 2),
+    ('B', 1, 2, 3),
+    ('sy', 1, 2, 3),
+    ('Yi', 1, 2, 0, 2),
+    ('Yq', 1, 0, 0, 1),
+    ('sw', 1, 0, 0, 1),
+    ('Yq', 1, 1, 0, 1),
+    ('sw', 1, 1, 0, 1),
+    ('Yi', 1, 2, 1, 2, 'V'),
+    ('Yq', 1, 2, 0, 2),
+    ('sw', 1, 2, 0, 2),
+    ('Yq', 1, 2, 1, 2),
+    ('sw', 1, 2, 1, 2),
+    ('ss', 1)]
+
+
+def tile_kronecker_sum_precondition_g5_kernel(
+    tc, grad, row_scale, left_t, col_scale, right_words, right_scales, diag_gain, trust, out_0, out_1, out_2
+):
+    nc = tc.nc
+    with ExitStack() as ctx:
+        keep = ctx.enter_context(tc.tile_pool(name="keep", bufs=1))
+        stage = ctx.enter_context(tc.tile_pool(name="stage", bufs=3))
+        psum = ctx.enter_context(tc.psum_pool(name="psum", bufs=1))
+        ctx.enter_context(tc.manual_schedule())
+
+        ident = keep.tile([P, P], F32, name="ident")
+        g_raw = keep.tile([P, GROUPS, CHUNKS, PACK, W], BF16, name="g_raw", align_bytes=64)
+        l_raw = keep.tile([P, GROUPS, GROUPS, PACK, W], BF16, name="l_raw", align_bytes=64)
+        r_words = keep.tile([P, CHUNKS, CHUNKS, 2 * W], U8, name="r_words", align_bytes=64)
+        r_scales = keep.tile([P, CHUNKS, N], U8, name="r_scales", align_bytes=64)
+        vec = {
+            "row": keep.tile([P, GROUPS, 16], BF16, name="row_v"),
+            "trust": keep.tile([P, GROUPS, 16], BF16, name="trust_v"),
+            "col": keep.tile([P, CHUNKS, 16], BF16, name="col_v"),
+            "diag": keep.tile([P, 2 * CHUNKS, 16], BF16, name="diag_v"),
+        }
+        row_f32 = keep.tile([P, GROUPS, PACK], F32, name="row_f32")
+        diag_all = keep.tile([P, N], BF16, name="diag_all", align_bytes=64)
+        x_codes = keep.tile([P, GROUPS, CHUNKS, W], U32, name="x_codes", align_bytes=64)
+        x_scales = keep.tile([P, GROUPS, CHUNKS, W], U8, name="x_scales", align_bytes=64)
+        z_codes = keep.tile([P, GROUPS, CHUNKS, W], U32, name="z_codes", align_bytes=64)
+        z_scales = keep.tile([P, GROUPS, CHUNKS, W], U8, name="z_scales", align_bytes=64)
+        l_codes = keep.tile([P, GROUPS, GROUPS, W], U32, name="l_codes", align_bytes=64)
+        l_scales = keep.tile([P, GROUPS, GROUPS, W], U8, name="l_scales", align_bytes=64)
+        y_f32 = keep.tile([P, GROUPS, CHUNKS, PACK, W], F32, name="y_f32", align_bytes=64)
+        y_codes = keep.tile([P, GROUPS, N], U32, name="y_codes", align_bytes=64)
+        y_scales = keep.tile([P, GROUPS, N], U8, name="y_scales", align_bytes=64)
+
+        queue = {"SP": nc.sync, "S": nc.scalar}
+        live = {}
+        count = {"turn": 0, "acc": 0}
+        passes_done = {}
+
+        def cols(c):
+            return slice(c * W, (c + 1) * W)
+
+        def turn_bank():
+            b = count["turn"] % TURN_BANKS
+            count["turn"] = count["turn"] + 1
+            return psum.tile([P, W], F32, name="turn%d" % b, tag="turn%d" % b)
+
+        def copy_on(e, out, in_):
+            if e == "S":
+                nc.scalar.copy(out=out, in_=in_)
+            else:
+                nc.vector.tensor_copy(out=out, in_=in_)
+
+        def load(what, q="SP"):
+            eng = queue[q]
+            kind = what[0]
+            if kind == "G":
+                g, c = what[1], what[2]
+                eng.dma_start(out=g_raw[:, g, c, :, :], in_=grad[cols(g), cols(c)].rearrange("(p t) w -> p t w", t=PACK))
+            elif kind == "L":
+                u, g = what[1], what[2]
+                eng.dma_start(out=l_raw[:, u, g, :, :], in_=left_t[cols(u), cols(g)].rearrange("(p t) w -> p t w", t=PACK))
+            elif kind == "R":
+                c = what[1]
+                eng.dma_start(
+                    out=r_words[:, c, :, :].bitcast(I32),
+                    in_=right_words[:, :, 2 * W * c : 2 * W * (c + 1)].rearrange("k p b -> p k b").bitcast(I32),
+                )
+            elif kind == "rs":
+                for q4 in range(4):
+                    eng.dma_start(
+                        out=r_scales[32 * q4 : 32 * q4 + 4, :, :].bitcast(I32),
+                        in_=right_scales[:, 4 * q4 : 4 * q4 + 4, :].rearrange("k r n -> r k n").bitcast(I32),
+                    )
+            elif what[1] == "diag":
+                eng.dma_start(out=vec["diag"][:, :, 0:2], in_=diag_gain.rearrange("(m p e) -> p m e", p=P, e=2))
+            else:
+                src = {"row": row_scale, "trust": trust, "col": col_scale}[what[1]]
+                eng.dma_start(out=vec[what[1]][:, :, 0:PACK], in_=src.rearrange("(g p t) -> p g t", p=P, t=PACK))
+
+        def spread_diag(h):
+            bank = turn_bank()
+            live["diag", h] = bank
+            words = vec["diag"][:].bitcast(F32)
+            for m in range(4 * h, min(4 * h + 4, 2 * CHUNKS)):
+                nc.tensor.transpose(bank[:, (m % 4) * P : (m % 4 + 1) * P], words[:, m, 0:1].to_broadcast([P, P]), ident[:])
+
+        def fetch_diag(h):
+            n = min(4 * h + 4, 2 * CHUNKS) * P - 4 * h * P
+            nc.scalar.copy(out=diag_all[:].bitcast(F32)[:, h * W : h * W + n], in_=live["diag", h][:, 0:n])
+
+        def turn(g, c, h):
+            bank = turn_bank()
+            live["turn", g, c, h] = bank
+            for tt in range(2):
+                words = g_raw[:, g, c, 2 * h + tt, :].bitcast(F32)
+                for u in range(2):
+                    at = (2 * u + tt) * P
+                    nc.tensor.transpose(bank[:, at : at + P], words[:, u : W // 2 : 2], ident[:])
+
+        def z_scale(g, c, h):
+            if ("z", g, c) not in live:
+                live["z", g, c] = stage.tile([P, PACK * W], BF16, name="z_bf", align_bytes=64)
+            half = live["z", g, c][:, h * 2 * W : (h + 1) * 2 * W]
+            nc.vector.tensor_tensor(
+                out=half.rearrange("p (r u e) -> p r u e", u=2, e=2),
+                in0=live["turn", g, c, h][:].bitcast(BF16).rearrange("p (u r e) -> p r u e", u=2, e=2),
+                in1=vec["col"][:, c, 0:PACK].rearrange("p (u e) -> p u e", u=2).unsqueeze(1).to_broadcast([P, 2 * P, 2, 2]),
+                op=ALU.mult,
+            )
+
+        def quantize(codes, scales, src):
+            nc.vector.quantize_mx(out=codes.bitcast(FP8X4), scales=scales, in_=src)
+
+        def x_scale(g, c, e="V"):
+            xs = stage.tile([P, PACK, W], BF16, name="x_rows", align_bytes=64)
+            live["xs", g, c] = xs
+            for t in range(PACK):
+                if e == "V":
+                    nc.vector.tensor_scalar(
+                        out=xs[:, t, :], in0=g_raw[:, g, c, t, :], scalar1=vec["row"][:, g, t : t + 1], scalar2=None, op0=ALU.mult
+                    )
+                else:
+                    nc.scalar.activation(out=xs[:, t, :], in_=g_raw[:, g, c, t, :], func=ACT.Copy, scale=row_f32[:, g, t : t + 1])
+
+        def x_weave(g, c, e="S"):
+            xb = stage.tile([P, PACK * W], BF16, name="x_bf", align_bytes=64)
+            live["xb", g, c] = xb
+            copy_on(
+                e,
+                xb[:].rearrange("p (c i t) -> p c t i", i=4, t=PACK),
+                live["xs", g, c][:].rearrange("p t (c i) -> p c t i", i=4),
+            )
+
+        def l_weave(u, g, e="S"):
+            lb = stage.tile([P, PACK * W], BF16, name="l_bf", align_bytes=64, bufs=2)
+            live["lb", u, g] = lb
+            copy_on(
+                e,
+                lb[:].rearrange("p (t m j) -> p m j t", t=PACK, j=PACK),
+                l_raw[:, u, g, :, :].rearrange("p j (m t) -> p m j t", t=PACK),
+            )
+
+        def diag_term(g, c, t):
+            nc.vector.scalar_tensor_tensor(
+                out=y_f32[:, g, c, t, :], in0=g_raw[:, g, c, t, :], scalar=vec["trust"][:, g, t : t + 1],
+                in1=diag_all[:, cols(c)], op0=ALU.mult, op1=ALU.mult,
+            )
+
+        def mx_pass(g, c, t, k):
+            if (g, c, t) not in passes_done:
+                b = count["acc"] % ACC_BANKS
+                count["acc"] = count["acc"] + 1
+                live["acc", g, c, t] = psum.tile([P, W], F32, name="acc%d" % b, tag="acc%d" % b)
+                passes_done[g, c, t] = 0
+            done = passes_done[g, c, t]
+            passes_done[g, c, t] = done + 1
+            rows = slice(t * P, (t + 1) * P)
+            if k < CHUNKS:
+                lhs, lhs_s = z_codes[:, g, k, rows], z_scales[:, g, k, rows]
+                rhs, rhs_s = r_words[:, c, k, :].bitcast(FP4X4), r_scales[:, k, cols(c)]
+            else:
+                u = k - CHUNKS
+                lhs, lhs_s = l_codes[:, u, g, rows], l_scales[:, u, g, rows]
+                rhs, rhs_s = x_codes[:, u, c, :].bitcast(FP8X4), x_scales[:, u, c, :]
+            nc.tensor.matmul_mx(
+                out=live["acc", g, c, t][:], lhsT=lhs.bitcast(FP8X4), lhsT_scale=lhs_s, rhs=rhs, rhs_scale=rhs_s,
+                start=(done == 0), stop=(done == CHUNKS + GROUPS - 1),
+            )
+
+        def finish(g, c, t):
+            nc.vector.scalar_tensor_tensor(
+                out=y_f32[:, g, c, t, :], in0=live["acc", g, c, t][:], scalar=vec["trust"][:, g, t : t + 1],
+                in1=y_f32[:, g, c, t, :], op0=ALU.mult, op1=ALU.add,
+            )
+
+        def store_y(g, c, t):
+            nc.sync.dma_start(
+                out=out_0[cols(g), cols(c)].rearrange("(p t) w -> p t w", t=PACK)[:, t, :], in_=y_f32[:, g, c, t, :]
+            )
+
+        def y_weave(g, c, h, n, e="S"):
+            if ("yb", g, c) not in live:
+                live["yb", g, c] = stage.tile([P, PACK * W], BF16, name="y_bf", align_bytes=64)
+            w = W // n
+            copy_on(
+                e,
+                live["yb", g, c][:, PACK * w * h : PACK * w * (h + 1)].rearrange("p (c i t) -> p c t i", i=4, t=PACK),
+                y_f32[:, g, c, :, w * h : w * (h + 1)].rearrange("p t (c i) -> p c t i", i=4),
+            )
+
+        def y_quantize(g, c, h, n):
+            w = W // n
+            at = slice(c * W + w * h, c * W + w * (h + 1))
+            quantize(y_codes[:, g, at], y_scales[:, g, at], live["yb", g, c][:, PACK * w * h : PACK * w * (h + 1)])
+
+        def store_words(g, c, h, n):
+            w = W // n
+            at = slice(c * W + w * h, c * W + w * (h + 1))
+            nc.sync.dma_start(
+                out=out_1[g].rearrange("p m t -> p (m t)").bitcast(I32)[:, at], in_=y_codes[:, g, at].bitcast(I32)
+            )
+
+        def store_scales(g):
+            for q4 in range(4):
+                nc.sync.dma_start(
+                    out=out_2[g, 4 * q4 : 4 * q4 + 4, :].bitcast(I32), in_=y_scales[32 * q4 : 32 * q4 + 4, g, :].bitcast(I32)
+                )
+
+        steps = {
+            "ident": lambda: make_identity(nc, ident[:]),
+            "memset": lambda: nc.vector.memset(r_scales[:].rearrange("p k n -> p (k n)").bitcast(I32), 0),
+            "rowf": lambda: nc.vector.tensor_copy(out=row_f32[:], in_=vec["row"][:, :, 0:PACK]),
+            "ld": load,
+            "TD": spread_diag,
+            "ED": fetch_diag,
+            "T": turn,
+            "Zm": z_scale,
+            "Zq": lambda g, c: quantize(z_codes[:, g, c, :], z_scales[:, g, c, :], live["z", g, c][:]),
+            "Xs": x_scale,
+            "Xi": x_weave,
+            "Xq": lambda g, c: quantize(x_codes[:, g, c, :], x_scales[:, g, c, :], live["xb", g, c][:]),
+            "Li": l_weave,
+            "Lq": lambda u, g: quantize(l_codes[:, u, g, :], l_scales[:, u, g, :], live["lb", u, g][:]),
+            "A": diag_term,
+            "M": mx_pass,
+            "B": finish,
+            "sy": store_y,
+            "Yi": y_weave,
+            "Yq": y_quantize,
+            "sw": store_words,
+            "ss": store_scales,
+        }
+        for step in ORDER:
+            steps[step[0]](*step[1:])

@@ -18,308 +18,29 @@ ACT = mybir.ActivationFunctionType
 
 P = 128
 PACK = 4
-W = 512
+W = P * PACK
 GROUPS = M // W
 CHUNKS = N // W
-ACC_BANKS = 6
-TURN_BANKS = 2
+QUADRANTS = 4
+VEC_PITCH = 16
+ALL_SLOTS = range(PACK)
 
-ORDER = [('ident',),
-    ('ld', ('v', 'diag'), 'S'),
-    ('ld', ('v', 'row'), 'S'),
-    ('ld', ('v', 'col'), 'S'),
-    ('ld', ('v', 'trust'), 'S'),
-    ('ld', ('G', 0, 0)),
-    ('ld', ('G', 0, 1)),
-    ('ld', ('L', 0, 0)),
-    ('ld', ('G', 1, 0)),
-    ('memset',),
-    ('ld', ('G', 0, 2)),
-    ('ld', ('R', 0)),
-    ('ld', ('rs',)),
-    ('ld', ('L', 1, 0)),
-    ('ld', ('G', 1, 1)),
-    ('ld', ('R', 1)),
-    ('ld', ('G', 1, 2)),
-    ('ld', ('L', 0, 1)),
-    ('ld', ('L', 1, 1)),
-    ('ld', ('R', 2)),
-    ('TD', 0),
-    ('ED', 0),
-    ('TD', 1),
-    ('ED', 1),
-    ('rowf',),
-    ('Xs', 0, 0),
-    ('T', 0, 0, 0),
-    ('T', 0, 0, 1),
-    ('Xi', 0, 0),
-    ('A', 0, 0, 0),
-    ('Zm', 0, 0, 0),
-    ('Zm', 0, 0, 1),
-    ('T', 0, 1, 0),
-    ('T', 0, 1, 1),
-    ('Li', 0, 0),
-    ('Xs', 1, 0),
-    ('Zq', 0, 0),
-    ('Zm', 0, 1, 0),
-    ('Zm', 0, 1, 1),
-    ('Xq', 0, 0),
-    ('Xi', 1, 0),
-    ('T', 0, 2, 0),
-    ('T', 0, 2, 1),
-    ('Zq', 0, 1),
-    ('Zm', 0, 2, 0),
-    ('Zm', 0, 2, 1),
-    ('Lq', 0, 0),
-    ('M', 0, 0, 0, 0),
-    ('M', 0, 0, 1, 0),
-    ('M', 0, 0, 2, 0),
-    ('M', 0, 0, 3, 0),
-    ('M', 0, 0, 0, 1),
-    ('M', 0, 0, 1, 1),
-    ('M', 0, 0, 2, 1),
-    ('M', 0, 0, 3, 1),
-    ('Li', 1, 0),
-    ('Zq', 0, 2),
-    ('Xs', 0, 1),
-    ('Xi', 0, 1),
-    ('A', 0, 0, 1),
-    ('M', 0, 0, 0, 3),
-    ('M', 0, 0, 1, 3),
-    ('M', 0, 0, 2, 3),
-    ('M', 0, 0, 3, 3),
-    ('M', 0, 0, 0, 2),
-    ('M', 0, 0, 1, 2),
-    ('M', 0, 0, 2, 2),
-    ('M', 0, 0, 3, 2),
-    ('T', 1, 0, 0),
-    ('T', 1, 0, 1),
-    ('Xq', 1, 0),
-    ('A', 0, 0, 2),
-    ('Xs', 1, 1),
-    ('Xi', 1, 1),
-    ('Lq', 1, 0),
-    ('A', 0, 0, 3),
-    ('M', 0, 1, 0, 0),
-    ('M', 0, 1, 0, 1),
-    ('M', 0, 1, 0, 2),
-    ('M', 0, 1, 1, 0),
-    ('M', 0, 1, 1, 1),
-    ('M', 0, 1, 1, 2),
-    ('M', 0, 0, 0, 4),
-    ('M', 0, 0, 1, 4),
-    ('M', 0, 0, 2, 4),
-    ('M', 0, 0, 3, 4),
-    ('Zm', 1, 0, 0),
-    ('Zm', 1, 0, 1),
-    ('Xq', 0, 1),
-    ('T', 1, 1, 0),
-    ('T', 1, 1, 1),
-    ('Xs', 0, 2, 'S'),
-    ('Xi', 0, 2),
-    ('B', 0, 0, 0),
-    ('sy', 0, 0, 0),
-    ('A', 0, 1, 0),
-    ('B', 0, 0, 1),
-    ('sy', 0, 0, 1),
-    ('Xq', 1, 1),
-    ('M', 0, 1, 0, 3),
-    ('M', 0, 1, 1, 3),
-    ('M', 0, 1, 0, 4),
-    ('M', 0, 1, 1, 4),
-    ('M', 0, 1, 2, 0),
-    ('M', 0, 1, 2, 1),
-    ('M', 0, 1, 2, 2),
-    ('M', 0, 1, 2, 3),
-    ('M', 0, 1, 2, 4),
-    ('B', 0, 0, 2),
-    ('sy', 0, 0, 2),
-    ('A', 0, 1, 1),
-    ('B', 0, 0, 3),
-    ('sy', 0, 0, 3),
-    ('M', 0, 1, 3, 0),
-    ('M', 0, 1, 3, 1),
-    ('M', 0, 1, 3, 2),
-    ('M', 0, 1, 3, 3),
-    ('M', 0, 1, 3, 4),
-    ('Zq', 1, 0),
-    ('Xs', 1, 2, 'S'),
-    ('Xi', 1, 2),
-    ('Zm', 1, 1, 0),
-    ('Zm', 1, 1, 1),
-    ('T', 1, 2, 0),
-    ('T', 1, 2, 1),
-    ('B', 0, 1, 0),
-    ('sy', 0, 1, 0),
-    ('Xq', 0, 2),
-    ('B', 0, 1, 1),
-    ('sy', 0, 1, 1),
-    ('A', 0, 1, 2),
-    ('M', 0, 2, 0, 0),
-    ('M', 0, 2, 0, 1),
-    ('M', 0, 2, 0, 2),
-    ('M', 0, 2, 0, 3),
-    ('M', 0, 2, 1, 0),
-    ('M', 0, 2, 1, 1),
-    ('M', 0, 2, 1, 2),
-    ('M', 0, 2, 1, 3),
-    ('Zq', 1, 1),
-    ('B', 0, 1, 2),
-    ('sy', 0, 1, 2),
-    ('A', 0, 1, 3),
-    ('M', 0, 2, 2, 0),
-    ('M', 0, 2, 2, 1),
-    ('M', 0, 2, 2, 2),
-    ('M', 0, 2, 2, 3),
-    ('Zm', 1, 2, 0),
-    ('B', 0, 1, 3),
-    ('sy', 0, 1, 3),
-    ('Zm', 1, 2, 1),
-    ('Li', 0, 1),
-    ('Xq', 1, 2),
-    ('M', 0, 2, 3, 0),
-    ('M', 0, 2, 3, 1),
-    ('M', 0, 2, 3, 2),
-    ('M', 0, 2, 3, 3),
-    ('M', 0, 2, 0, 4),
-    ('M', 0, 2, 1, 4),
-    ('M', 0, 2, 2, 4),
-    ('M', 0, 2, 3, 4),
-    ('A', 0, 2, 0),
-    ('Zq', 1, 2),
-    ('A', 0, 2, 1),
-    ('Li', 1, 1),
-    ('Lq', 0, 1),
-    ('M', 1, 0, 0, 0),
-    ('M', 1, 0, 0, 1),
-    ('M', 1, 0, 0, 2),
-    ('M', 1, 0, 0, 3),
-    ('M', 1, 0, 1, 0),
-    ('M', 1, 0, 1, 1),
-    ('M', 1, 0, 1, 2),
-    ('M', 1, 0, 1, 3),
-    ('B', 0, 2, 0),
-    ('sy', 0, 2, 0),
-    ('A', 0, 2, 2),
-    ('B', 0, 2, 1),
-    ('sy', 0, 2, 1),
-    ('Lq', 1, 1),
-    ('Yi', 0, 0, 0, 1),
-    ('M', 1, 0, 0, 4),
-    ('M', 1, 0, 1, 4),
-    ('M', 1, 0, 2, 0),
-    ('M', 1, 0, 2, 1),
-    ('M', 1, 0, 2, 2),
-    ('M', 1, 0, 2, 3),
-    ('M', 1, 0, 2, 4),
-    ('A', 0, 2, 3),
-    ('B', 0, 2, 2),
-    ('sy', 0, 2, 2),
-    ('A', 1, 0, 0),
-    ('B', 0, 2, 3),
-    ('sy', 0, 2, 3),
-    ('M', 1, 0, 3, 0),
-    ('M', 1, 0, 3, 1),
-    ('M', 1, 0, 3, 2),
-    ('M', 1, 0, 3, 3),
-    ('M', 1, 0, 3, 4),
-    ('Yi', 0, 1, 0, 1),
-    ('Yi', 0, 2, 0, 1),
-    ('A', 1, 0, 1),
-    ('B', 1, 0, 0),
-    ('sy', 1, 0, 0),
-    ('M', 1, 1, 0, 0),
-    ('M', 1, 1, 0, 1),
-    ('M', 1, 1, 0, 2),
-    ('M', 1, 1, 0, 3),
-    ('M', 1, 1, 0, 4),
-    ('A', 1, 0, 2),
-    ('Yq', 0, 0, 0, 1),
-    ('sw', 0, 0, 0, 1),
-    ('B', 1, 0, 1),
-    ('sy', 1, 0, 1),
-    ('M', 1, 1, 1, 0),
-    ('M', 1, 1, 1, 1),
-    ('M', 1, 1, 1, 2),
-    ('M', 1, 1, 1, 3),
-    ('M', 1, 1, 1, 4),
-    ('A', 1, 0, 3),
-    ('B', 1, 0, 2),
-    ('sy', 1, 0, 2),
-    ('M', 1, 1, 2, 0),
-    ('M', 1, 1, 2, 1),
-    ('M', 1, 1, 2, 2),
-    ('M', 1, 1, 2, 3),
-    ('M', 1, 1, 2, 4),
-    ('A', 1, 1, 0),
-    ('B', 1, 0, 3),
-    ('sy', 1, 0, 3),
-    ('M', 1, 1, 3, 0),
-    ('M', 1, 1, 3, 1),
-    ('M', 1, 1, 3, 2),
-    ('M', 1, 1, 3, 3),
-    ('M', 1, 1, 3, 4),
-    ('Yi', 1, 0, 0, 1),
-    ('A', 1, 1, 1),
-    ('B', 1, 1, 0),
-    ('sy', 1, 1, 0),
-    ('M', 1, 2, 0, 0),
-    ('M', 1, 2, 0, 1),
-    ('M', 1, 2, 0, 2),
-    ('M', 1, 2, 0, 3),
-    ('M', 1, 2, 0, 4),
-    ('A', 1, 1, 2),
-    ('Yq', 0, 1, 0, 1),
-    ('sw', 0, 1, 0, 1),
-    ('B', 1, 1, 1),
-    ('sy', 1, 1, 1),
-    ('M', 1, 2, 1, 0),
-    ('M', 1, 2, 1, 1),
-    ('M', 1, 2, 1, 2),
-    ('M', 1, 2, 1, 3),
-    ('M', 1, 2, 1, 4),
-    ('A', 1, 1, 3),
-    ('B', 1, 1, 2),
-    ('sy', 1, 1, 2),
-    ('M', 1, 2, 2, 0),
-    ('M', 1, 2, 2, 1),
-    ('M', 1, 2, 2, 2),
-    ('M', 1, 2, 2, 3),
-    ('M', 1, 2, 2, 4),
-    ('A', 1, 2, 0),
-    ('B', 1, 1, 3),
-    ('sy', 1, 1, 3),
-    ('M', 1, 2, 3, 0),
-    ('M', 1, 2, 3, 1),
-    ('M', 1, 2, 3, 2),
-    ('M', 1, 2, 3, 3),
-    ('M', 1, 2, 3, 4),
-    ('Yi', 1, 1, 0, 1),
-    ('A', 1, 2, 1),
-    ('B', 1, 2, 0),
-    ('sy', 1, 2, 0),
-    ('A', 1, 2, 2),
-    ('Yq', 0, 2, 0, 1),
-    ('sw', 0, 2, 0, 1),
-    ('B', 1, 2, 1),
-    ('sy', 1, 2, 1),
-    ('A', 1, 2, 3),
-    ('ss', 0),
-    ('B', 1, 2, 2),
-    ('sy', 1, 2, 2),
-    ('B', 1, 2, 3),
-    ('sy', 1, 2, 3),
-    ('Yi', 1, 2, 0, 2),
-    ('Yq', 1, 0, 0, 1),
-    ('sw', 1, 0, 0, 1),
-    ('Yq', 1, 1, 0, 1),
-    ('sw', 1, 1, 0, 1),
-    ('Yi', 1, 2, 1, 2, 'V'),
-    ('Yq', 1, 2, 0, 2),
-    ('sw', 1, 2, 0, 2),
-    ('Yq', 1, 2, 1, 2),
-    ('sw', 1, 2, 1, 2),
-    ('ss', 1)]
+RIGHT = (0, 1, 2)
+LEFT = (3, 4)
+ALL_PASSES = RIGHT + LEFT
+
+PSUM_BANKS = 8
+EARLY_BANKS = 6
+EARLY_TILES = 12
+
+
+def bank_of(g, c, t):
+    i = (g * CHUNKS + c) * PACK + t
+    return i % EARLY_BANKS if i < EARLY_TILES else (i - EARLY_TILES + EARLY_BANKS) % PSUM_BANKS
+
+
+def part(i, width=W):
+    return slice(i * width, (i + 1) * width)
 
 
 def tile_kronecker_sum_precondition_g5_kernel(
@@ -328,7 +49,7 @@ def tile_kronecker_sum_precondition_g5_kernel(
     nc = tc.nc
     with ExitStack() as ctx:
         keep = ctx.enter_context(tc.tile_pool(name="keep", bufs=1))
-        stage = ctx.enter_context(tc.tile_pool(name="stage", bufs=3))
+        stage = ctx.enter_context(tc.tile_pool(name="stage", bufs=1))
         psum = ctx.enter_context(tc.psum_pool(name="psum", bufs=1))
         ctx.enter_context(tc.manual_schedule())
 
@@ -337,13 +58,11 @@ def tile_kronecker_sum_precondition_g5_kernel(
         l_raw = keep.tile([P, GROUPS, GROUPS, PACK, W], BF16, name="l_raw", align_bytes=64)
         r_words = keep.tile([P, CHUNKS, CHUNKS, 2 * W], U8, name="r_words", align_bytes=64)
         r_scales = keep.tile([P, CHUNKS, N], U8, name="r_scales", align_bytes=64)
-        vec = {
-            "row": keep.tile([P, GROUPS, 16], BF16, name="row_v"),
-            "trust": keep.tile([P, GROUPS, 16], BF16, name="trust_v"),
-            "col": keep.tile([P, CHUNKS, 16], BF16, name="col_v"),
-            "diag": keep.tile([P, 2 * CHUNKS, 16], BF16, name="diag_v"),
-        }
-        row_f32 = keep.tile([P, GROUPS, PACK], F32, name="row_f32")
+        row_v = keep.tile([P, GROUPS, VEC_PITCH], BF16, name="row_v")
+        trust_v = keep.tile([P, GROUPS, VEC_PITCH], BF16, name="trust_v")
+        col_v = keep.tile([P, CHUNKS, VEC_PITCH], BF16, name="col_v")
+        diag_v = keep.tile([P, CHUNKS, VEC_PITCH], BF16, name="diag_v")
+        trust_f32 = keep.tile([P, GROUPS, PACK], F32, name="trust_f32")
         diag_all = keep.tile([P, N], BF16, name="diag_all", align_bytes=64)
         x_codes = keep.tile([P, GROUPS, CHUNKS, W], U32, name="x_codes", align_bytes=64)
         x_scales = keep.tile([P, GROUPS, CHUNKS, W], U8, name="x_scales", align_bytes=64)
@@ -355,204 +74,330 @@ def tile_kronecker_sum_precondition_g5_kernel(
         y_codes = keep.tile([P, GROUPS, N], U32, name="y_codes", align_bytes=64)
         y_scales = keep.tile([P, GROUPS, N], U8, name="y_scales", align_bytes=64)
 
-        queue = {"SP": nc.sync, "S": nc.scalar}
-        live = {}
-        count = {"turn": 0, "acc": 0}
+        on_scalar, on_vector = nc.scalar.copy, nc.vector.tensor_copy
+        tiles = {}
         passes_done = {}
 
-        def cols(c):
-            return slice(c * W, (c + 1) * W)
+        def in_bank(key, bank):
+            tiles[key] = psum.tile([P, W], F32, name="bank%d" % bank)
+            return tiles[key]
 
-        def turn_bank():
-            b = count["turn"] % TURN_BANKS
-            count["turn"] = count["turn"] + 1
-            return psum.tile([P, W], F32, name="turn%d" % b, tag="turn%d" % b)
+        def in_buffer(key, buf, shape, dtype):
+            tiles[key] = stage.tile(shape, dtype, name="buffer%d" % buf, align_bytes=64)
+            return tiles[key]
 
-        def copy_on(e, out, in_):
-            if e == "S":
-                nc.scalar.copy(out=out, in_=in_)
-            else:
-                nc.vector.tensor_copy(out=out, in_=in_)
+        def by_slot(rows):
+            return rows.rearrange("(p t) w -> p t w", t=PACK)
 
-        def load(what, q="SP"):
-            eng = queue[q]
-            kind = what[0]
-            if kind == "G":
-                g, c = what[1], what[2]
-                eng.dma_start(out=g_raw[:, g, c, :, :], in_=grad[cols(g), cols(c)].rearrange("(p t) w -> p t w", t=PACK))
-            elif kind == "L":
-                u, g = what[1], what[2]
-                eng.dma_start(out=l_raw[:, u, g, :, :], in_=left_t[cols(u), cols(g)].rearrange("(p t) w -> p t w", t=PACK))
-            elif kind == "R":
-                c = what[1]
-                eng.dma_start(
-                    out=r_words[:, c, :, :].bitcast(I32),
-                    in_=right_words[:, :, 2 * W * c : 2 * W * (c + 1)].rearrange("k p b -> p k b").bitcast(I32),
+        def load_vector(tile, vector):
+            nc.scalar.dma_start(out=tile[:, :, 0:PACK], in_=vector.rearrange("(k p t) -> p k t", p=P, t=PACK))
+
+        def load_grad(g, c, slots=slice(0, PACK)):
+            nc.sync.dma_start(out=g_raw[:, g, c, slots, :], in_=by_slot(grad[part(g), part(c)])[:, slots, :])
+
+        def load_left(u, g):
+            nc.sync.dma_start(out=l_raw[:, u, g, :, :], in_=by_slot(left_t[part(u), part(g)]))
+
+        def load_right_words(c):
+            nc.sync.dma_start(
+                out=r_words[:, c, :, :].bitcast(I32),
+                in_=right_words[:, :, part(c, 2 * W)].rearrange("k p b -> p k b").bitcast(I32),
+            )
+
+        def load_right_scales():
+            for q in range(QUADRANTS):
+                nc.sync.dma_start(
+                    out=r_scales[32 * q : 32 * q + 4, :, :].bitcast(I32),
+                    in_=right_scales[:, part(q, 4), :].rearrange("k r n -> r k n").bitcast(I32),
                 )
-            elif kind == "rs":
-                for q4 in range(4):
-                    eng.dma_start(
-                        out=r_scales[32 * q4 : 32 * q4 + 4, :, :].bitcast(I32),
-                        in_=right_scales[:, 4 * q4 : 4 * q4 + 4, :].rearrange("k r n -> r k n").bitcast(I32),
-                    )
-            elif what[1] == "diag":
-                eng.dma_start(out=vec["diag"][:, :, 0:2], in_=diag_gain.rearrange("(m p e) -> p m e", p=P, e=2))
-            else:
-                src = {"row": row_scale, "trust": trust, "col": col_scale}[what[1]]
-                eng.dma_start(out=vec[what[1]][:, :, 0:PACK], in_=src.rearrange("(g p t) -> p g t", p=P, t=PACK))
 
-        def spread_diag(h):
-            bank = turn_bank()
-            live["diag", h] = bank
-            words = vec["diag"][:].bitcast(F32)
-            for m in range(4 * h, min(4 * h + 4, 2 * CHUNKS)):
-                nc.tensor.transpose(bank[:, (m % 4) * P : (m % 4 + 1) * P], words[:, m, 0:1].to_broadcast([P, P]), ident[:])
-
-        def fetch_diag(h):
-            n = min(4 * h + 4, 2 * CHUNKS) * P - 4 * h * P
-            nc.scalar.copy(out=diag_all[:].bitcast(F32)[:, h * W : h * W + n], in_=live["diag", h][:, 0:n])
-
-        def turn(g, c, h):
-            bank = turn_bank()
-            live["turn", g, c, h] = bank
-            for tt in range(2):
-                words = g_raw[:, g, c, 2 * h + tt, :].bitcast(F32)
+        def spread_diag(chunks, bank):
+            spread = in_bank(("diag", chunks), bank)
+            words = diag_v[:].bitcast(F32)
+            for i, c in enumerate(chunks):
                 for u in range(2):
-                    at = (2 * u + tt) * P
-                    nc.tensor.transpose(bank[:, at : at + P], words[:, u : W // 2 : 2], ident[:])
+                    nc.tensor.transpose(spread[:, part(2 * i + u, P)], words[:, c, u : u + 1].to_broadcast([P, P]), ident[:])
 
-        def z_scale(g, c, h):
-            if ("z", g, c) not in live:
-                live["z", g, c] = stage.tile([P, PACK * W], BF16, name="z_bf", align_bytes=64)
-            half = live["z", g, c][:, h * 2 * W : (h + 1) * 2 * W]
-            nc.vector.tensor_tensor(
-                out=half.rearrange("p (r u e) -> p r u e", u=2, e=2),
-                in0=live["turn", g, c, h][:].bitcast(BF16).rearrange("p (u r e) -> p r u e", u=2, e=2),
-                in1=vec["col"][:, c, 0:PACK].rearrange("p (u e) -> p u e", u=2).unsqueeze(1).to_broadcast([P, 2 * P, 2, 2]),
-                op=ALU.mult,
+        def fetch_diag(chunks):
+            n_words = len(chunks) * W // 2
+            first = chunks[0] * W // 2
+            nc.scalar.copy(
+                out=diag_all[:].bitcast(F32)[:, first : first + n_words].rearrange("p (c n u) -> p c n u", n=P, u=2),
+                in_=tiles["diag", chunks][:, 0:n_words].rearrange("p (c u n) -> p c n u", n=P, u=2),
             )
 
-        def quantize(codes, scales, src):
-            nc.vector.quantize_mx(out=codes.bitcast(FP8X4), scales=scales, in_=src)
+        def quantize(codes, scales, values):
+            nc.vector.quantize_mx(out=codes.bitcast(FP8X4), scales=scales, in_=values)
 
-        def x_scale(g, c, e="V"):
-            xs = stage.tile([P, PACK, W], BF16, name="x_rows", align_bytes=64)
-            live["xs", g, c] = xs
-            for t in range(PACK):
-                if e == "V":
-                    nc.vector.tensor_scalar(
-                        out=xs[:, t, :], in0=g_raw[:, g, c, t, :], scalar1=vec["row"][:, g, t : t + 1], scalar2=None, op0=ALU.mult
-                    )
-                else:
-                    nc.scalar.activation(out=xs[:, t, :], in_=g_raw[:, g, c, t, :], func=ACT.Copy, scale=row_f32[:, g, t : t + 1])
+        def turn(g, c, half, bank):
+            turned = in_bank(("turned", g, c, half), bank)
+            for s in range(2):
+                words = g_raw[:, g, c, 2 * half + s, :].bitcast(F32)
+                for u in range(2):
+                    nc.tensor.transpose(turned[:, part(2 * u + s, P)], words[:, u : W // 2 : 2], ident[:])
 
-        def x_weave(g, c, e="S"):
-            xb = stage.tile([P, PACK * W], BF16, name="x_bf", align_bytes=64)
-            live["xb", g, c] = xb
-            copy_on(
-                e,
-                xb[:].rearrange("p (c i t) -> p c t i", i=4, t=PACK),
-                live["xs", g, c][:].rearrange("p t (c i) -> p c t i", i=4),
+        def z_scale(g, c, halves, buf=None):
+            z = tiles["z", g, c] if buf is None else in_buffer(("z", g, c), buf, [P, PACK * W], BF16)
+            col = col_v[:, c, 0:PACK].rearrange("p (u e) -> p u e", u=2).unsqueeze(1).to_broadcast([P, 2 * P, 2, 2])
+            for half in halves:
+                nc.vector.tensor_tensor(
+                    out=z[:, part(half, 2 * W)].rearrange("p (r u e) -> p r u e", u=2, e=2),
+                    in0=tiles["turned", g, c, half][:].bitcast(BF16).rearrange("p (u r e) -> p r u e", u=2, e=2),
+                    in1=col,
+                    op=ALU.mult,
+                )
+
+        def z_quantize(g, c):
+            quantize(z_codes[:, g, c, :], z_scales[:, g, c, :], tiles["z", g, c][:])
+
+        def x_scale(g, c, slots, buf=None):
+            rows = tiles["x_rows", g, c] if buf is None else in_buffer(("x_rows", g, c), buf, [P, PACK, W], BF16)
+            for t in slots:
+                nc.vector.tensor_scalar(
+                    out=rows[:, t, :], in0=g_raw[:, g, c, t, :], scalar1=row_v[:, g, t : t + 1], scalar2=None, op0=ALU.mult
+                )
+
+        def x_weave(g, c, buf, copy=on_scalar):
+            x = in_buffer(("x", g, c), buf, [P, PACK * W], BF16)
+            copy(out=x[:].rearrange("p (w t) -> p w t", t=PACK), in_=tiles["x_rows", g, c][:].rearrange("p t w -> p w t"))
+
+        def x_quantize(g, c):
+            quantize(x_codes[:, g, c, :], x_scales[:, g, c, :], tiles["x", g, c][:])
+
+        def l_weave(u, g, buf):
+            woven = in_buffer(("l", u, g), buf, [P, PACK * W], BF16)
+            nc.scalar.copy(
+                out=woven[:].rearrange("p (t m j) -> p m t j", t=PACK, j=PACK),
+                in_=l_raw[:, u, g, :, :].rearrange("p j (m t) -> p m t j", t=PACK),
             )
 
-        def l_weave(u, g, e="S"):
-            lb = stage.tile([P, PACK * W], BF16, name="l_bf", align_bytes=64, bufs=2)
-            live["lb", u, g] = lb
-            copy_on(
-                e,
-                lb[:].rearrange("p (t m j) -> p m j t", t=PACK, j=PACK),
-                l_raw[:, u, g, :, :].rearrange("p j (m t) -> p m j t", t=PACK),
-            )
-
-        def diag_term(g, c, t):
-            nc.vector.scalar_tensor_tensor(
-                out=y_f32[:, g, c, t, :], in0=g_raw[:, g, c, t, :], scalar=vec["trust"][:, g, t : t + 1],
-                in1=diag_all[:, cols(c)], op0=ALU.mult, op1=ALU.mult,
-            )
+        def l_quantize(u, g):
+            quantize(l_codes[:, u, g, :], l_scales[:, u, g, :], tiles["l", u, g][:])
 
         def mx_pass(g, c, t, k):
-            if (g, c, t) not in passes_done:
-                b = count["acc"] % ACC_BANKS
-                count["acc"] = count["acc"] + 1
-                live["acc", g, c, t] = psum.tile([P, W], F32, name="acc%d" % b, tag="acc%d" % b)
-                passes_done[g, c, t] = 0
-            done = passes_done[g, c, t]
+            done = passes_done.get((g, c, t), 0)
             passes_done[g, c, t] = done + 1
-            rows = slice(t * P, (t + 1) * P)
-            if k < CHUNKS:
-                lhs, lhs_s = z_codes[:, g, k, rows], z_scales[:, g, k, rows]
-                rhs, rhs_s = r_words[:, c, k, :].bitcast(FP4X4), r_scales[:, k, cols(c)]
+            acc = tiles["acc", g, c, t] if done else in_bank(("acc", g, c, t), bank_of(g, c, t))
+            if k in RIGHT:
+                lhs, lhs_scale = z_codes[:, g, k, part(t, P)], z_scales[:, g, k, part(t, P)]
+                rhs, rhs_scale = r_words[:, c, k, :].bitcast(FP4X4), r_scales[:, k, part(c)]
             else:
-                u = k - CHUNKS
-                lhs, lhs_s = l_codes[:, u, g, rows], l_scales[:, u, g, rows]
-                rhs, rhs_s = x_codes[:, u, c, :].bitcast(FP8X4), x_scales[:, u, c, :]
+                u = LEFT.index(k)
+                lhs, lhs_scale = l_codes[:, u, g, part(t, P)], l_scales[:, u, g, part(t, P)]
+                rhs, rhs_scale = x_codes[:, u, c, :].bitcast(FP8X4), x_scales[:, u, c, :]
             nc.tensor.matmul_mx(
-                out=live["acc", g, c, t][:], lhsT=lhs.bitcast(FP8X4), lhsT_scale=lhs_s, rhs=rhs, rhs_scale=rhs_s,
-                start=(done == 0), stop=(done == CHUNKS + GROUPS - 1),
+                out=acc[:], lhsT=lhs.bitcast(FP8X4), lhsT_scale=lhs_scale, rhs=rhs, rhs_scale=rhs_scale,
+                start=(done == 0), stop=(done == len(ALL_PASSES) - 1),
             )
 
-        def finish(g, c, t):
-            nc.vector.scalar_tensor_tensor(
-                out=y_f32[:, g, c, t, :], in0=live["acc", g, c, t][:], scalar=vec["trust"][:, g, t : t + 1],
-                in1=y_f32[:, g, c, t, :], op0=ALU.mult, op1=ALU.add,
-            )
+        def passes_across(g, c, slots, passes):
+            for k in passes:
+                for t in slots:
+                    mx_pass(g, c, t, k)
 
-        def store_y(g, c, t):
-            nc.sync.dma_start(
-                out=out_0[cols(g), cols(c)].rearrange("(p t) w -> p t w", t=PACK)[:, t, :], in_=y_f32[:, g, c, t, :]
-            )
+        def passes_along(g, c, slots, passes):
+            for t in slots:
+                for k in passes:
+                    mx_pass(g, c, t, k)
 
-        def y_weave(g, c, h, n, e="S"):
-            if ("yb", g, c) not in live:
-                live["yb", g, c] = stage.tile([P, PACK * W], BF16, name="y_bf", align_bytes=64)
-            w = W // n
-            copy_on(
-                e,
-                live["yb", g, c][:, PACK * w * h : PACK * w * (h + 1)].rearrange("p (c i t) -> p c t i", i=4, t=PACK),
-                y_f32[:, g, c, :, w * h : w * (h + 1)].rearrange("p t (c i) -> p c t i", i=4),
-            )
+        def diag_term(g, c, slots):
+            for t in slots:
+                nc.vector.scalar_tensor_tensor(
+                    out=y_f32[:, g, c, t, :], in0=g_raw[:, g, c, t, :], scalar=trust_v[:, g, t : t + 1],
+                    in1=diag_all[:, part(c)], op0=ALU.mult, op1=ALU.mult,
+                )
+                tiles["term", g, c, t] = y_f32[:, g, c, t, :]
 
-        def y_quantize(g, c, h, n):
-            w = W // n
-            at = slice(c * W + w * h, c * W + w * (h + 1))
-            quantize(y_codes[:, g, at], y_scales[:, g, at], live["yb", g, c][:, PACK * w * h : PACK * w * (h + 1)])
-
-        def store_words(g, c, h, n):
-            w = W // n
-            at = slice(c * W + w * h, c * W + w * (h + 1))
-            nc.sync.dma_start(
-                out=out_1[g].rearrange("p m t -> p (m t)").bitcast(I32)[:, at], in_=y_codes[:, g, at].bitcast(I32)
-            )
-
-        def store_scales(g):
-            for q4 in range(4):
-                nc.sync.dma_start(
-                    out=out_2[g, 4 * q4 : 4 * q4 + 4, :].bitcast(I32), in_=y_scales[32 * q4 : 32 * q4 + 4, g, :].bitcast(I32)
+        def trust_rows(g, c, slots):
+            for t in slots:
+                nc.scalar.activation(
+                    out=y_f32[:, g, c, t, :], in_=g_raw[:, g, c, t, :], func=ACT.Copy, scale=trust_f32[:, g, t : t + 1]
                 )
 
-        steps = {
-            "ident": lambda: make_identity(nc, ident[:]),
-            "memset": lambda: nc.vector.memset(r_scales[:].rearrange("p k n -> p (k n)").bitcast(I32), 0),
-            "rowf": lambda: nc.vector.tensor_copy(out=row_f32[:], in_=vec["row"][:, :, 0:PACK]),
-            "ld": load,
-            "TD": spread_diag,
-            "ED": fetch_diag,
-            "T": turn,
-            "Zm": z_scale,
-            "Zq": lambda g, c: quantize(z_codes[:, g, c, :], z_scales[:, g, c, :], live["z", g, c][:]),
-            "Xs": x_scale,
-            "Xi": x_weave,
-            "Xq": lambda g, c: quantize(x_codes[:, g, c, :], x_scales[:, g, c, :], live["xb", g, c][:]),
-            "Li": l_weave,
-            "Lq": lambda u, g: quantize(l_codes[:, u, g, :], l_scales[:, u, g, :], live["lb", u, g][:]),
-            "A": diag_term,
-            "M": mx_pass,
-            "B": finish,
-            "sy": store_y,
-            "Yi": y_weave,
-            "Yq": y_quantize,
-            "sw": store_words,
-            "ss": store_scales,
-        }
-        for step in ORDER:
-            steps[step[0]](*step[1:])
+        def diag_term_gpsimd(g, c, slots, buf):
+            terms = in_buffer(("terms", g, c, slots), buf, [P, len(slots), W], F32)
+            for i, t in enumerate(slots):
+                nc.gpsimd.tensor_tensor(
+                    out=terms[:, i, :], in0=y_f32[:, g, c, t, :], in1=diag_all[:, part(c)], op=ALU.mult
+                )
+                tiles["term", g, c, t] = terms[:, i, :]
+
+        def finish(g, c, slots):
+            for t in slots:
+                nc.vector.scalar_tensor_tensor(
+                    out=y_f32[:, g, c, t, :], in0=tiles["acc", g, c, t][:], scalar=trust_v[:, g, t : t + 1],
+                    in1=tiles["term", g, c, t], op0=ALU.mult, op1=ALU.add,
+                )
+                nc.sync.dma_start(out=by_slot(out_0[part(g), part(c)])[:, t, :], in_=y_f32[:, g, c, t, :])
+
+        def y_weave(g, c, buf, i=0, n=1, copy=on_scalar):
+            y = tiles["y", g, c] if buf is None else in_buffer(("y", g, c), buf, [P, PACK * W], BF16)
+            copy(
+                out=y[:, part(i, PACK * W // n)].rearrange("p (b w t) -> p b t w", w=4, t=PACK),
+                in_=y_f32[:, g, c, :, part(i, W // n)].rearrange("p t (b w) -> p b t w", w=4),
+            )
+
+        def y_quantize(g, c, i=0, n=1):
+            columns = part(c * n + i, W // n)
+            quantize(y_codes[:, g, columns], y_scales[:, g, columns], tiles["y", g, c][:, part(i, PACK * W // n)])
+            nc.sync.dma_start(
+                out=out_1[g].rearrange("p m t -> p (m t)").bitcast(I32)[:, columns], in_=y_codes[:, g, columns].bitcast(I32)
+            )
+
+        def store_scales(g, queues):
+            for q in range(QUADRANTS):
+                queues[q].dma_start(
+                    out=out_2[g, part(q, 4), :].bitcast(I32), in_=y_scales[32 * q : 32 * q + 4, g, :].bitcast(I32)
+                )
+
+
+        nc.vector.memset(r_scales[:].rearrange("p k n -> p (k n)").bitcast(I32), 0)
+        make_identity(nc, ident[:])
+        load_vector(row_v, row_scale)
+        load_vector(diag_v, diag_gain)
+        load_vector(col_v, col_scale)
+        load_vector(trust_v, trust)
+        load_grad(0, 0, slice(0, 2))
+        load_grad(0, 0, slice(2, 4))
+        load_grad(0, 1)
+        load_left(0, 0)
+        load_right_scales()
+        load_right_words(0)
+        load_grad(0, 2)
+        load_left(1, 0)
+        load_grad(1, 0)
+        load_grad(1, 1)
+        load_right_words(1)
+        load_grad(1, 2)
+        load_right_words(2)
+        load_left(0, 1)
+        load_left(1, 1)
+
+        x_scale(0, 0, (0, 1), buf=0)
+        turn(0, 0, 0, bank=6)
+        spread_diag((0, 1), bank=0)
+        turn(0, 0, 1, bank=7)
+        x_scale(0, 0, (2, 3))
+        x_weave(0, 0, 3)
+        fetch_diag((0, 1))
+        z_scale(0, 0, (0,), buf=8)
+        nc.vector.tensor_copy(out=trust_f32[:], in_=trust_v[:, :, 0:PACK])
+        turn(0, 1, 0, bank=4)
+        turn(0, 1, 1, bank=5)
+        x_scale(0, 1, ALL_SLOTS, buf=1)
+        z_scale(0, 0, (1,))
+        x_weave(0, 1, 4, copy=on_vector)
+        z_quantize(0, 0)
+        spread_diag((2,), bank=6)
+        l_weave(0, 0, 6)
+        fetch_diag((2,))
+        z_scale(0, 1, (1, 0), buf=9)
+        x_quantize(0, 0)
+        z_quantize(0, 1)
+        passes_across(0, 0, ALL_SLOTS, (0, 1))
+
+        l_quantize(0, 0)
+        diag_term(0, 0, (0,))
+        x_scale(0, 2, ALL_SLOTS, buf=1)
+        x_quantize(0, 1)
+        turn(0, 2, 0, bank=6)
+        turn(0, 2, 1, bank=7)
+        passes_across(0, 0, ALL_SLOTS, (3,))
+        trust_rows(0, 2, (0, 1))
+        l_weave(1, 0, 7)
+        diag_term(0, 0, (1,))
+        z_scale(0, 2, (0,), buf=10)
+        x_scale(1, 0, ALL_SLOTS, buf=2)
+        x_weave(1, 0, 5)
+        z_scale(0, 2, (1,))
+        turn(1, 0, 0, bank=6)
+        turn(1, 0, 1, bank=7)
+        x_scale(1, 1, ALL_SLOTS, buf=0)
+        z_quantize(0, 2)
+        passes_along(0, 1, (0, 1), (0, 1, 3))
+        passes_across(0, 0, ALL_SLOTS, (2,))
+        passes_across(0, 1, (0, 1), (2,))
+        x_weave(1, 1, 3)
+        diag_term(0, 0, (2,))
+        z_scale(1, 0, (1,), buf=11)
+        l_quantize(1, 0)
+        x_quantize(1, 0)
+        diag_term(0, 0, (3,))
+        z_scale(1, 0, (0,))
+        passes_across(0, 0, ALL_SLOTS, (4,))
+
+        turn(1, 1, 0, bank=6)
+        turn(1, 1, 1, bank=7)
+        x_weave(0, 2, 4)
+        x_scale(1, 2, ALL_SLOTS, buf=2)
+        trust_rows(0, 2, (2, 3))
+        x_weave(1, 2, 5)
+        x_quantize(1, 1)
+        diag_term_gpsimd(0, 2, (0, 1), buf=3)
+        passes_across(0, 1, (0, 1), (4,))
+        finish(0, 0, (1, 0))
+        passes_along(0, 1, (2, 3), ALL_PASSES)
+        z_scale(1, 1, (1, 0), buf=12)
+        turn(1, 2, 0, bank=6)
+        turn(1, 2, 1, bank=7)
+        finish(0, 0, (3, 2))
+
+        x_quantize(0, 2)
+        diag_term(0, 1, (0, 1, 2))
+        x_quantize(1, 2)
+        diag_term_gpsimd(0, 2, (2, 3), buf=5)
+        passes_along(0, 2, (0, 1), ALL_PASSES)
+        finish(0, 1, (1, 0))
+        z_scale(1, 2, (1, 0), buf=13)
+        finish(0, 1, (2,))
+        l_weave(0, 1, 6)
+        passes_along(0, 2, (2, 3), ALL_PASSES)
+        z_quantize(1, 0)
+        z_quantize(1, 1)
+        z_quantize(1, 2)
+        l_weave(1, 1, 7)
+        diag_term(0, 1, (3,))
+        l_quantize(0, 1)
+
+        passes_along(1, 0, (0, 1), (0, 1, 2, 3))
+        diag_term(1, 0, (0,))
+        trust_rows(1, 1, (2, 3))
+        trust_rows(1, 2, (0, 1))
+        l_quantize(1, 1)
+        diag_term_gpsimd(1, 1, (2, 3), buf=7)
+        y_weave(0, 0, 8)
+        passes_across(1, 0, (0, 1), (4,))
+        finish(0, 1, (3,))
+        passes_along(1, 0, (2, 3), ALL_PASSES)
+        finish(0, 2, (3, 2, 1, 0))
+
+        passes_along(1, 1, ALL_SLOTS, ALL_PASSES)
+        y_weave(0, 1, 9)
+        diag_term(1, 0, (1, 2, 3))
+        diag_term(1, 1, (0,))
+        y_quantize(0, 0)
+        diag_term_gpsimd(1, 2, (0, 1), buf=8)
+        finish(1, 0, (3, 2, 1, 0))
+        finish(1, 1, (0,))
+
+        passes_along(1, 2, ALL_SLOTS, ALL_PASSES)
+        y_weave(0, 2, 10)
+        diag_term(1, 1, (1,))
+        y_quantize(0, 1)
+        y_weave(1, 0, 14)
+        y_quantize(0, 2)
+        store_scales(0, [nc.sync] * QUADRANTS)
+        finish(1, 1, (3, 2, 1))
+        y_weave(1, 1, 15)
+        finish(1, 2, (0,))
+        diag_term(1, 2, (2,))
+        y_quantize(1, 0)
+        diag_term(1, 2, (3,))
+        finish(1, 2, (1, 2, 3))
+
+        y_weave(1, 2, 16, 0, 2)
+        y_quantize(1, 1)
+        y_weave(1, 2, None, 1, 2, copy=on_vector)
+        y_quantize(1, 2, 0, 2)
+        y_quantize(1, 2, 1, 2)
+        store_scales(1, [nc.sync, nc.sync, nc.scalar, nc.scalar])

from contextlib import ExitStack

import concourse.mybir as mybir
from concourse.masks import make_identity

M, N = 1024, 1536
FLOPS = 2 * M * M * N + 2 * M * N * N

F32 = mybir.dt.float32
BF16 = mybir.dt.bfloat16
I32 = mybir.dt.int32
U32 = mybir.dt.uint32
U8 = mybir.dt.uint8
FP8X4 = mybir.dt.float8_e4m3fn_x4
FP4X4 = mybir.dt.float4_e2m1fn_x4
ALU = mybir.AluOpType
ACT = mybir.ActivationFunctionType

P = 128
PACK = 4
W = P * PACK
GROUPS = M // W
CHUNKS = N // W
QUADRANTS = 4
VEC_PITCH = 16
ALL_SLOTS = range(PACK)

RIGHT = (0, 1, 2)
LEFT = (3, 4)
ALL_PASSES = RIGHT + LEFT

PSUM_BANKS = 8
EARLY_BANKS = 6
EARLY_TILES = 12


def bank_of(g, c, t):
    i = (g * CHUNKS + c) * PACK + t
    return i % EARLY_BANKS if i < EARLY_TILES else (i - EARLY_TILES + EARLY_BANKS) % PSUM_BANKS


def part(i, width=W):
    return slice(i * width, (i + 1) * width)


def tile_kronecker_sum_precondition_g5_kernel(
    tc, grad, row_scale, left_t, col_scale, right_words, right_scales, diag_gain, trust, out_0, out_1, out_2
):
    nc = tc.nc
    with ExitStack() as ctx:
        keep = ctx.enter_context(tc.tile_pool(name="keep", bufs=1))
        stage = ctx.enter_context(tc.tile_pool(name="stage", bufs=1))
        psum = ctx.enter_context(tc.psum_pool(name="psum", bufs=1))
        ctx.enter_context(tc.manual_schedule())

        ident = keep.tile([P, P], F32, name="ident")
        g_raw = keep.tile([P, GROUPS, CHUNKS, PACK, W], BF16, name="g_raw", align_bytes=64)
        l_raw = keep.tile([P, GROUPS, GROUPS, PACK, W], BF16, name="l_raw", align_bytes=64)
        r_words = keep.tile([P, CHUNKS, CHUNKS, 2 * W], U8, name="r_words", align_bytes=64)
        r_scales = keep.tile([P, CHUNKS, N], U8, name="r_scales", align_bytes=64)
        row_v = keep.tile([P, GROUPS, VEC_PITCH], BF16, name="row_v")
        trust_v = keep.tile([P, GROUPS, VEC_PITCH], BF16, name="trust_v")
        col_v = keep.tile([P, CHUNKS, VEC_PITCH], BF16, name="col_v")
        diag_v = keep.tile([P, CHUNKS, VEC_PITCH], BF16, name="diag_v")
        trust_f32 = keep.tile([P, GROUPS, PACK], F32, name="trust_f32")
        diag_all = keep.tile([P, N], BF16, name="diag_all", align_bytes=64)
        x_codes = keep.tile([P, GROUPS, CHUNKS, W], U32, name="x_codes", align_bytes=64)
        x_scales = keep.tile([P, GROUPS, CHUNKS, W], U8, name="x_scales", align_bytes=64)
        z_codes = keep.tile([P, GROUPS, CHUNKS, W], U32, name="z_codes", align_bytes=64)
        z_scales = keep.tile([P, GROUPS, CHUNKS, W], U8, name="z_scales", align_bytes=64)
        l_codes = keep.tile([P, GROUPS, GROUPS, W], U32, name="l_codes", align_bytes=64)
        l_scales = keep.tile([P, GROUPS, GROUPS, W], U8, name="l_scales", align_bytes=64)
        y_f32 = keep.tile([P, GROUPS, CHUNKS, PACK, W], F32, name="y_f32", align_bytes=64)
        y_codes = keep.tile([P, GROUPS, N], U32, name="y_codes", align_bytes=64)
        y_scales = keep.tile([P, GROUPS, N], U8, name="y_scales", align_bytes=64)

        on_scalar, on_vector = nc.scalar.copy, nc.vector.tensor_copy
        tiles = {}
        passes_done = {}

        def in_bank(key, bank):
            tiles[key] = psum.tile([P, W], F32, name="bank%d" % bank)
            return tiles[key]

        def in_buffer(key, buf, shape, dtype):
            tiles[key] = stage.tile(shape, dtype, name="buffer%d" % buf, align_bytes=64)
            return tiles[key]

        def by_slot(rows):
            return rows.rearrange("(p t) w -> p t w", t=PACK)

        def load_vector(tile, vector):
            nc.scalar.dma_start(out=tile[:, :, 0:PACK], in_=vector.rearrange("(k p t) -> p k t", p=P, t=PACK))

        def load_grad(g, c, slots=slice(0, PACK)):
            nc.sync.dma_start(out=g_raw[:, g, c, slots, :], in_=by_slot(grad[part(g), part(c)])[:, slots, :])

        def load_left(u, g):
            nc.sync.dma_start(out=l_raw[:, u, g, :, :], in_=by_slot(left_t[part(u), part(g)]))

        def load_right_words(c):
            nc.sync.dma_start(
                out=r_words[:, c, :, :].bitcast(I32),
                in_=right_words[:, :, part(c, 2 * W)].rearrange("k p b -> p k b").bitcast(I32),
            )

        def load_right_scales():
            for q in range(QUADRANTS):
                nc.sync.dma_start(
                    out=r_scales[32 * q : 32 * q + 4, :, :].bitcast(I32),
                    in_=right_scales[:, part(q, 4), :].rearrange("k r n -> r k n").bitcast(I32),
                )

        def spread_diag(chunks, bank):
            spread = in_bank(("diag", chunks), bank)
            words = diag_v[:].bitcast(F32)
            for i, c in enumerate(chunks):
                for u in range(2):
                    nc.tensor.transpose(spread[:, part(2 * i + u, P)], words[:, c, u : u + 1].to_broadcast([P, P]), ident[:])

        def fetch_diag(chunks):
            n_words = len(chunks) * W // 2
            first = chunks[0] * W // 2
            nc.scalar.copy(
                out=diag_all[:].bitcast(F32)[:, first : first + n_words].rearrange("p (c n u) -> p c n u", n=P, u=2),
                in_=tiles["diag", chunks][:, 0:n_words].rearrange("p (c u n) -> p c n u", n=P, u=2),
            )

        def quantize(codes, scales, values):
            nc.vector.quantize_mx(out=codes.bitcast(FP8X4), scales=scales, in_=values)

        def turn(g, c, half, bank):
            turned = in_bank(("turned", g, c, half), bank)
            for s in range(2):
                words = g_raw[:, g, c, 2 * half + s, :].bitcast(F32)
                for u in range(2):
                    nc.tensor.transpose(turned[:, part(2 * u + s, P)], words[:, u : W // 2 : 2], ident[:])

        def z_scale(g, c, halves, buf=None):
            z = tiles["z", g, c] if buf is None else in_buffer(("z", g, c), buf, [P, PACK * W], BF16)
            col = col_v[:, c, 0:PACK].rearrange("p (u e) -> p u e", u=2).unsqueeze(1).to_broadcast([P, 2 * P, 2, 2])
            for half in halves:
                nc.vector.tensor_tensor(
                    out=z[:, part(half, 2 * W)].rearrange("p (r u e) -> p r u e", u=2, e=2),
                    in0=tiles["turned", g, c, half][:].bitcast(BF16).rearrange("p (u r e) -> p r u e", u=2, e=2),
                    in1=col,
                    op=ALU.mult,
                )

        def z_quantize(g, c):
            quantize(z_codes[:, g, c, :], z_scales[:, g, c, :], tiles["z", g, c][:])

        def x_scale(g, c, slots, buf=None):
            rows = tiles["x_rows", g, c] if buf is None else in_buffer(("x_rows", g, c), buf, [P, PACK, W], BF16)
            for t in slots:
                nc.vector.tensor_scalar(
                    out=rows[:, t, :], in0=g_raw[:, g, c, t, :], scalar1=row_v[:, g, t : t + 1], scalar2=None, op0=ALU.mult
                )

        def x_weave(g, c, buf, copy=on_scalar):
            x = in_buffer(("x", g, c), buf, [P, PACK * W], BF16)
            copy(out=x[:].rearrange("p (w t) -> p w t", t=PACK), in_=tiles["x_rows", g, c][:].rearrange("p t w -> p w t"))

        def x_quantize(g, c):
            quantize(x_codes[:, g, c, :], x_scales[:, g, c, :], tiles["x", g, c][:])

        def l_weave(u, g, buf):
            woven = in_buffer(("l", u, g), buf, [P, PACK * W], BF16)
            nc.scalar.copy(
                out=woven[:].rearrange("p (t m j) -> p m t j", t=PACK, j=PACK),
                in_=l_raw[:, u, g, :, :].rearrange("p j (m t) -> p m t j", t=PACK),
            )

        def l_quantize(u, g):
            quantize(l_codes[:, u, g, :], l_scales[:, u, g, :], tiles["l", u, g][:])

        def mx_pass(g, c, t, k):
            done = passes_done.get((g, c, t), 0)
            passes_done[g, c, t] = done + 1
            acc = tiles["acc", g, c, t] if done else in_bank(("acc", g, c, t), bank_of(g, c, t))
            if k in RIGHT:
                lhs, lhs_scale = z_codes[:, g, k, part(t, P)], z_scales[:, g, k, part(t, P)]
                rhs, rhs_scale = r_words[:, c, k, :].bitcast(FP4X4), r_scales[:, k, part(c)]
            else:
                u = LEFT.index(k)
                lhs, lhs_scale = l_codes[:, u, g, part(t, P)], l_scales[:, u, g, part(t, P)]
                rhs, rhs_scale = x_codes[:, u, c, :].bitcast(FP8X4), x_scales[:, u, c, :]
            nc.tensor.matmul_mx(
                out=acc[:], lhsT=lhs.bitcast(FP8X4), lhsT_scale=lhs_scale, rhs=rhs, rhs_scale=rhs_scale,
                start=(done == 0), stop=(done == len(ALL_PASSES) - 1),
            )

        def passes_across(g, c, slots, passes):
            for k in passes:
                for t in slots:
                    mx_pass(g, c, t, k)

        def passes_along(g, c, slots, passes):
            for t in slots:
                for k in passes:
                    mx_pass(g, c, t, k)

        def diag_term(g, c, slots):
            for t in slots:
                nc.vector.scalar_tensor_tensor(
                    out=y_f32[:, g, c, t, :], in0=g_raw[:, g, c, t, :], scalar=trust_v[:, g, t : t + 1],
                    in1=diag_all[:, part(c)], op0=ALU.mult, op1=ALU.mult,
                )
                tiles["term", g, c, t] = y_f32[:, g, c, t, :]

        def trust_rows(g, c, slots):
            for t in slots:
                nc.scalar.activation(
                    out=y_f32[:, g, c, t, :], in_=g_raw[:, g, c, t, :], func=ACT.Copy, scale=trust_f32[:, g, t : t + 1]
                )

        def diag_term_gpsimd(g, c, slots, buf):
            terms = in_buffer(("terms", g, c, slots), buf, [P, len(slots), W], F32)
            for i, t in enumerate(slots):
                nc.gpsimd.tensor_tensor(
                    out=terms[:, i, :], in0=y_f32[:, g, c, t, :], in1=diag_all[:, part(c)], op=ALU.mult
                )
                tiles["term", g, c, t] = terms[:, i, :]

        def finish(g, c, slots):
            for t in slots:
                nc.vector.scalar_tensor_tensor(
                    out=y_f32[:, g, c, t, :], in0=tiles["acc", g, c, t][:], scalar=trust_v[:, g, t : t + 1],
                    in1=tiles["term", g, c, t], op0=ALU.mult, op1=ALU.add,
                )
                nc.sync.dma_start(out=by_slot(out_0[part(g), part(c)])[:, t, :], in_=y_f32[:, g, c, t, :])

        def y_weave(g, c, buf, i=0, n=1, copy=on_scalar):
            y = tiles["y", g, c] if buf is None else in_buffer(("y", g, c), buf, [P, PACK * W], BF16)
            copy(
                out=y[:, part(i, PACK * W // n)].rearrange("p (b w t) -> p b t w", w=4, t=PACK),
                in_=y_f32[:, g, c, :, part(i, W // n)].rearrange("p t (b w) -> p b t w", w=4),
            )

        def y_quantize(g, c, i=0, n=1):
            columns = part(c * n + i, W // n)
            quantize(y_codes[:, g, columns], y_scales[:, g, columns], tiles["y", g, c][:, part(i, PACK * W // n)])
            nc.sync.dma_start(
                out=out_1[g].rearrange("p m t -> p (m t)").bitcast(I32)[:, columns], in_=y_codes[:, g, columns].bitcast(I32)
            )

        def store_scales(g, queues):
            for q in range(QUADRANTS):
                queues[q].dma_start(
                    out=out_2[g, part(q, 4), :].bitcast(I32), in_=y_scales[32 * q : 32 * q + 4, g, :].bitcast(I32)
                )


        nc.vector.memset(r_scales[:].rearrange("p k n -> p (k n)").bitcast(I32), 0)
        make_identity(nc, ident[:])
        load_vector(row_v, row_scale)
        load_vector(diag_v, diag_gain)
        load_vector(col_v, col_scale)
        load_vector(trust_v, trust)
        load_grad(0, 0, slice(0, 2))
        load_grad(0, 0, slice(2, 4))
        load_grad(0, 1)
        load_left(0, 0)
        load_right_scales()
        load_right_words(0)
        load_grad(0, 2)
        load_left(1, 0)
        load_grad(1, 0)
        load_grad(1, 1)
        load_right_words(1)
        load_grad(1, 2)
        load_right_words(2)
        load_left(0, 1)
        load_left(1, 1)

        x_scale(0, 0, (0, 1), buf=0)
        turn(0, 0, 0, bank=6)
        spread_diag((0, 1), bank=0)
        turn(0, 0, 1, bank=7)
        x_scale(0, 0, (2, 3))
        x_weave(0, 0, 3)
        fetch_diag((0, 1))
        z_scale(0, 0, (0,), buf=8)
        nc.vector.tensor_copy(out=trust_f32[:], in_=trust_v[:, :, 0:PACK])
        turn(0, 1, 0, bank=4)
        turn(0, 1, 1, bank=5)
        x_scale(0, 1, ALL_SLOTS, buf=1)
        z_scale(0, 0, (1,))
        x_weave(0, 1, 4, copy=on_vector)
        z_quantize(0, 0)
        spread_diag((2,), bank=6)
        l_weave(0, 0, 6)
        fetch_diag((2,))
        z_scale(0, 1, (1, 0), buf=9)
        x_quantize(0, 0)
        z_quantize(0, 1)
        passes_across(0, 0, ALL_SLOTS, (0, 1))

        l_quantize(0, 0)
        diag_term(0, 0, (0,))
        x_scale(0, 2, ALL_SLOTS, buf=1)
        x_quantize(0, 1)
        turn(0, 2, 0, bank=6)
        turn(0, 2, 1, bank=7)
        passes_across(0, 0, ALL_SLOTS, (3,))
        trust_rows(0, 2, (0, 1))
        l_weave(1, 0, 7)
        diag_term(0, 0, (1,))
        z_scale(0, 2, (0,), buf=10)
        x_scale(1, 0, ALL_SLOTS, buf=2)
        x_weave(1, 0, 5)
        z_scale(0, 2, (1,))
        turn(1, 0, 0, bank=6)
        turn(1, 0, 1, bank=7)
        x_scale(1, 1, ALL_SLOTS, buf=0)
        z_quantize(0, 2)
        passes_along(0, 1, (0, 1), (0, 1, 3))
        passes_across(0, 0, ALL_SLOTS, (2,))
        passes_across(0, 1, (0, 1), (2,))
        x_weave(1, 1, 3)
        diag_term(0, 0, (2,))
        z_scale(1, 0, (1,), buf=11)
        l_quantize(1, 0)
        x_quantize(1, 0)
        diag_term(0, 0, (3,))
        z_scale(1, 0, (0,))
        passes_across(0, 0, ALL_SLOTS, (4,))

        turn(1, 1, 0, bank=6)
        turn(1, 1, 1, bank=7)
        x_weave(0, 2, 4)
        x_scale(1, 2, ALL_SLOTS, buf=2)
        trust_rows(0, 2, (2, 3))
        x_weave(1, 2, 5)
        x_quantize(1, 1)
        diag_term_gpsimd(0, 2, (0, 1), buf=3)
        passes_across(0, 1, (0, 1), (4,))
        finish(0, 0, (1, 0))
        passes_along(0, 1, (2, 3), ALL_PASSES)
        z_scale(1, 1, (1, 0), buf=12)
        turn(1, 2, 0, bank=6)
        turn(1, 2, 1, bank=7)
        finish(0, 0, (3, 2))

        x_quantize(0, 2)
        diag_term(0, 1, (0, 1, 2))
        x_quantize(1, 2)
        diag_term_gpsimd(0, 2, (2, 3), buf=5)
        passes_along(0, 2, (0, 1), ALL_PASSES)
        finish(0, 1, (1, 0))
        z_scale(1, 2, (1, 0), buf=13)
        finish(0, 1, (2,))
        l_weave(0, 1, 6)
        passes_along(0, 2, (2, 3), ALL_PASSES)
        z_quantize(1, 0)
        z_quantize(1, 1)
        z_quantize(1, 2)
        l_weave(1, 1, 7)
        diag_term(0, 1, (3,))
        l_quantize(0, 1)

        passes_along(1, 0, (0, 1), (0, 1, 2, 3))
        diag_term(1, 0, (0,))
        trust_rows(1, 1, (2, 3))
        trust_rows(1, 2, (0, 1))
        l_quantize(1, 1)
        diag_term_gpsimd(1, 1, (2, 3), buf=7)
        y_weave(0, 0, 8)
        passes_across(1, 0, (0, 1), (4,))
        finish(0, 1, (3,))
        passes_along(1, 0, (2, 3), ALL_PASSES)
        finish(0, 2, (3, 2, 1, 0))

        passes_along(1, 1, ALL_SLOTS, ALL_PASSES)
        y_weave(0, 1, 9)
        diag_term(1, 0, (1, 2, 3))
        diag_term(1, 1, (0,))
        y_quantize(0, 0)
        diag_term_gpsimd(1, 2, (0, 1), buf=8)
        finish(1, 0, (3, 2, 1, 0))
        finish(1, 1, (0,))

        passes_along(1, 2, ALL_SLOTS, ALL_PASSES)
        y_weave(0, 2, 10)
        diag_term(1, 1, (1,))
        y_quantize(0, 1)
        y_weave(1, 0, 14)
        y_quantize(0, 2)
        store_scales(0, [nc.sync] * QUADRANTS)
        finish(1, 1, (3, 2, 1))
        y_weave(1, 1, 15)
        finish(1, 2, (0,))
        diag_term(1, 2, (2,))
        y_quantize(1, 0)
        diag_term(1, 2, (3,))
        finish(1, 2, (1, 2, 3))

        y_weave(1, 2, 16, 0, 2)
        y_quantize(1, 1)
        y_weave(1, 2, None, 1, 2, copy=on_vector)
        y_quantize(1, 2, 0, 2)
        y_quantize(1, 2, 1, 2)
        store_scales(1, [nc.sync, nc.sync, nc.scalar, nc.scalar])
